import numpy as np
import ml_dtypes


def mxq(x, axis, fmt="e4m3"):
    dtype, down = {"e4m3": (ml_dtypes.float8_e4m3fn, 7), "e5m2": (ml_dtypes.float8_e5m2, 14)}[fmt]
    v = np.moveaxis(np.asarray(x, np.float32).astype(ml_dtypes.bfloat16).astype(np.float64), axis, -1)
    blocks = v.reshape(v.shape[:-1] + (-1, 32))
    amax = np.abs(blocks).max(-1, keepdims=True)
    byte = np.maximum(np.where(amax > 0, np.frexp(amax)[1] - 1 + 127, 0) - down, 1)
    scale = np.exp2(byte - 127.0)
    codes = (blocks / scale).astype(np.float32).astype(dtype).astype(np.float64)
    return np.moveaxis((codes * scale).reshape(v.shape), -1, axis)


WIDE = False


def mx_kscale(k):
    if not WIDE:
        return np.ones(k)
    levels = np.array([10, -10, 5, -5, 0])
    if k % 512:
        return np.exp2(np.random.permutation(np.resize(levels, k // 32))).repeat(32)
    a = np.empty((k // 512, 16))
    for p in range(k // 512):
        a[p, :8] = np.random.permutation(np.resize(levels, 8))
        for g in range(8):
            far = levels[np.abs(levels - a[p, g]) >= 10]
            a[p, g + 8] = far[np.random.randint(len(far))]
    return np.exp2(a.ravel()).repeat(32)


def f64(x):
    return np.asarray(x).astype(np.float64)


def striped(idx):
    return np.tile(idx.reshape(-1, 16).T, (8, 1)).astype(np.uint16)


def unstriped(offs):
    return offs[:16].T.reshape(-1).astype(np.int64)


def pack_weight(w):
    k, n = w.shape
    w = f64(np.asarray(w, np.float32).astype(ml_dtypes.bfloat16)).reshape(k // 32, 32, n)
    amax = np.abs(w).max(1)
    byte = np.clip(np.where(amax > 0, np.frexp(amax)[1] - 1 + 127 - 7, 1), 1, 254)
    scaled = (w * np.exp2(127.0 - byte)[:, None, :]).reshape(k, n).astype(np.float32)
    words = np.ascontiguousarray(scaled.reshape(k // 512, 128, 4, n).transpose(0, 1, 3, 2)).astype(ml_dtypes.float8_e4m3fn).view(np.uint8)
    return words, np.ascontiguousarray(byte.astype(np.uint8).reshape(k // 512, 16, n))


def unpack_weight(words, scales):
    g, p, n, _ = words.shape
    vals = np.ascontiguousarray(words).view(ml_dtypes.float8_e4m3fn).astype(np.float64) * np.repeat(np.exp2(scales.astype(np.float64) - 127.0), 8, axis=1)[..., None]
    return vals.transpose(0, 1, 3, 2).reshape(g * 512, n)


K, T, E, C, N = 1024, 768, 12, 128, 384


def by_expert(wq, xq):
    return np.concatenate([wq[e].T @ xq[:, e * C:(e + 1) * C] for e in range(E)], axis=1)


def setup_inputs():
    n = np.random.standard_normal
    s = mx_kscale(K)[:, None]
    first = np.random.permutation(np.repeat(np.arange(E), T // E))
    second = (first + 1 + np.random.permutation(np.repeat(np.arange(E - 1), -(-T // (E - 1)))[:T])) % E
    while np.bincount(second, minlength=E).max() != T // E:
        load = np.bincount(second, minlength=E); hi, lo = int(load.argmax()), int(load.argmin())
        t = np.flatnonzero((second == hi) & (first != lo))[0]; second[t] = lo
    slot_token = np.empty(E * C, np.int64); pos = np.empty((2, T), np.int64); fill = np.zeros(E, np.int64)
    place = np.stack([np.random.permutation(C) for _ in range(E)])
    for r, deal in enumerate((first, second)):
        for t in np.random.permutation(T):
            e = deal[t]; j = e * C + place[e, fill[e]]; fill[e] += 1; slot_token[j] = t; pos[r, t] = j
    g = np.random.uniform(0.2, 0.8, T)
    packed = [pack_weight(m) for m in n((E, K, N)) / np.sqrt(K) / s[None]]
    return {
        "xT": (n((K, T)) * s).astype(np.float32),
        "w_words": np.stack([m[0] for m in packed]),
        "w_scales": np.stack([m[1] for m in packed]),
        "gate": np.stack([np.tile(g, (N, 1)), np.tile(1.0 - g, (N, 1))]).astype(np.float32),
        "offs": striped(slot_token),
        "pos1": striped(pos[0]),
        "pos2": striped(pos[1]),
    }


def reference(xT, w_words, w_scales, gate, offs, pos1, pos2):
    idx = unstriped(offs)
    xq = mxq(f64(xT)[:, idx], 0, "e4m3")
    w = np.stack([unpack_weight(w_words[e], w_scales[e]) for e in range(E)])
    y = by_expert(w, xq)
    return f64(gate[0]) * y[:, unstriped(pos1)] + f64(gate[1]) * y[:, unstriped(pos2)]

@@ -1,0 +1,183 @@
+from contextlib import ExitStack
+
+import concourse.mybir as mybir
+from concourse.masks import make_identity
+
+K, T, E, C, N = 1024, 768, 12, 128, 384
+SLOTS = E * C
+P = 128
+FLOPS = 2 * K * N * SLOTS
+
+F32 = mybir.dt.float32
+BF16 = mybir.dt.bfloat16
+I32 = mybir.dt.int32
+U32 = mybir.dt.uint32
+U16 = mybir.dt.uint16
+U8 = mybir.dt.uint8
+FP8X4 = mybir.dt.float8_e4m3fn_x4
+MULT = mybir.AluOpType.mult
+
+PASSES = 2
+BLOCKS = N // P
+X_CHUNKS = ((0, 512), (512, 768))
+SLICE = 512
+SLICES = SLOTS // SLICE
+W_LOADS_A = ((0, 2, 0, 3), (2, 4, 0, 3), (4, 6, 0, 3), (6, 12, 0, 1))
+W_LOADS_B = ((6, 12, 1, 2),)
+W_LOADS_C = ((6, 12, 2, 3),)
+
+
+def tile_routed_moe_kernel(tc, xT, w_words, w_scales, gate, offs, pos1, pos2, out):
+    nc = tc.nc
+    with ExitStack() as ctx:
+        lists = ctx.enter_context(tc.tile_pool(name="lists", bufs=1))
+        keep = ctx.enter_context(tc.tile_pool(name="keep", bufs=1))
+        work = ctx.enter_context(tc.tile_pool(name="work", bufs=3))
+        psum = ctx.enter_context(tc.psum_pool(name="psum", bufs=8))
+
+        offs_t = lists.tile([P, SLOTS // 16], U16, name="offs_t")
+        pos1_t = lists.tile([P, T // 16], U16, name="pos1_t")
+        pos2_t = lists.tile([P, T // 16], U16, name="pos2_t")
+
+        x_bytes = keep.tile([P, T], U8, name="x_bytes", align_bytes=64)
+        nc.gpsimd.memset(x_bytes[:], 0)
+        w_bytes = keep.tile([P, E * PASSES, N], U8, name="w_bytes", align_bytes=64)
+        nc.gpsimd.memset(w_bytes[:].rearrange("p a n -> p (a n)").bitcast(I32), 0)
+
+        ident = keep.tile([P, P], F32, name="ident")
+        make_identity(nc, ident[:])
+
+        raw = {}
+        for a in range(PASSES):
+            rows = xT[a * 512 : (a + 1) * 512, :].rearrange("(p t) n -> p t n", t=4)
+            for c, (c0, c1) in enumerate(X_CHUNKS):
+                raw[a, c] = keep.tile([P, 4, c1 - c0], F32, name=f"raw_{a}_{c}")
+                nc.sync.dma_start(raw[a, c][:], rows[:, :, c0:c1])
+            if a == 0:
+                nc.sync.dma_start(offs_t[:], offs)
+
+        for q in range(4):
+            nc.sync.dma_start(
+                w_bytes[32 * q : 32 * q + 4, :, :].bitcast(I32),
+                w_scales[:, :, 4 * q : 4 * q + 4, :].rearrange("e a q n -> q (e a) n").bitcast(I32),
+            )
+
+        w_at = {}
+
+        def load_weights(loads):
+            for e0, e1, b0, b1 in loads:
+                w = keep.tile([P, (e1 - e0) * PASSES, (b1 - b0) * P * 4], U8, name=f"w_{e0}_{b0}", align_bytes=64)
+                nc.sync.dma_start(
+                    w[:], w_words[e0:e1, :, :, b0 * P : b1 * P, :].rearrange("e a p n r -> p (e a) (n r)")
+                )
+                for e in range(e0, e1):
+                    for b in range(b0, b1):
+                        w_at[e, b] = (w, (e - e0) * PASSES, (b - b0) * P * 4)
+
+        gate_t = {}
+
+        def load_gate(b):
+            gate_t[b] = keep.tile([P, 2, T], F32, name=f"gate_{b}")
+            nc.sync.dma_start(gate_t[b][:], gate[:, b * P : (b + 1) * P, :].rearrange("s p t -> p s t"))
+
+        load_weights(W_LOADS_A)
+        nc.sync.dma_start(pos1_t[:], pos1)
+        nc.sync.dma_start(pos2_t[:], pos2)
+        load_gate(0)
+        load_weights(W_LOADS_B)
+        load_gate(1)
+        load_weights(W_LOADS_C)
+        load_gate(2)
+
+        x_words = [keep.tile([P, T], U32, name=f"x_words_{a}", align_bytes=64) for a in range(PASSES)]
+        inter = [keep.tile([P, T, 4], BF16, name=f"inter_{a}", align_bytes=64) for a in range(PASSES)]
+
+        def interleave(engine, a, c, lo, hi):
+            c0 = X_CHUNKS[c][0]
+            dst = inter[a][:, c0 + lo : c0 + hi, :]
+            src = raw[a, c][:, :, lo:hi].rearrange("p t n -> p n t")
+            if engine == "scalar":
+                nc.scalar.copy(out=dst, in_=src)
+            else:
+                nc.vector.tensor_copy(out=dst, in_=src)
+
+        def quantise(a, c):
+            c0, c1 = X_CHUNKS[c]
+            nc.vector.quantize_mx(
+                out=x_words[a][:, c0:c1].bitcast(FP8X4),
+                scales=x_bytes[4 * a : P, c0:c1],
+                in_=inter[a][:, c0:c1, :].rearrange("p n t -> p (n t)"),
+            )
+
+        s_words = {}
+        s_bytes = {}
+
+        def gather_words(a, s):
+            s_words[a, s] = keep.tile([P, SLICE], U32, name=f"s_words_{a}_{s}", align_bytes=64)
+            nc.vector.tensor_copy(
+                s_words[a, s][:], x_words[a][:].indirect(offs_t[:, s * SLICE // 16 : (s + 1) * SLICE // 16])
+            )
+
+        def gather_bytes(s):
+            s_bytes[s] = keep.tile([P, SLICE], U8, name=f"s_bytes_{s}", align_bytes=64)
+            nc.vector.tensor_copy(
+                s_bytes[s][:], x_bytes[:].indirect(offs_t[:, s * SLICE // 16 : (s + 1) * SLICE // 16])
+            )
+
+        interleave("scalar", 0, 0, 0, 192)
+        interleave("vector", 0, 0, 192, 512)
+        interleave("scalar", 0, 1, 0, 96)
+        quantise(0, 0)
+        interleave("vector", 0, 1, 96, 256)
+        quantise(0, 1)
+        interleave("scalar", 1, 0, 0, 256)
+        interleave("scalar", 1, 0, 256, 512)
+        for s in range(SLICES):
+            gather_words(0, s)
+        interleave("scalar", 1, 1, 0, 128)
+        interleave("vector", 1, 1, 128, 256)
+        quantise(1, 0)
+        quantise(1, 1)
+
+        sums = [keep.tile([P, SLOTS], F32, name=f"sums_{b}") for b in range(BLOCKS)]
+
+        for s in range(SLICES):
+            gather_bytes(s)
+            gather_words(1, s)
+            for b in range(BLOCKS):
+                bank = psum.tile([P, SLICE], F32, name="bank")
+                for i in range(SLICE // C):
+                    e = s * (SLICE // C) + i
+                    w, row, col = w_at[e, b]
+                    cols = slice(i * C, (i + 1) * C)
+                    for a in range(PASSES):
+                        nc.tensor.matmul_mx(
+                            out=bank[:, cols],
+                            lhsT=w[:, row + a, col : col + 4 * P].bitcast(FP8X4),
+                            lhsT_scale=w_bytes[:, 2 * e + a, b * P : (b + 1) * P],
+                            rhs=s_words[a, s][:, cols].bitcast(FP8X4),
+                            rhs_scale=s_bytes[s][4 * a : P, cols],
+                            start=(a == 0),
+                            stop=(a == PASSES - 1),
+                        )
+                nc.scalar.copy(out=sums[b][:, s * SLICE : (s + 1) * SLICE], in_=bank[:])
+
+        PIECES = {0: (0, 768), 1: (0, 768), 2: (0, 384, 768)}
+        for b in range(BLOCKS):
+            edges = PIECES[b]
+            for t0, t1 in zip(edges[:-1], edges[1:]):
+                n = t1 - t0
+                first = work.tile([P, n], F32, name=f"first_{n}")
+                second = work.tile([P, n], F32, name=f"second_{n}")
+                total = work.tile([P, n], F32, name=f"total_{n}")
+                nc.vector.tensor_tensor(first[:], sums[b][:].indirect(pos1_t[:, t0 // 16 : t1 // 16]), gate_t[b][:, 0, t0:t1], MULT)
+                nc.vector.tensor_tensor(second[:], sums[b][:].indirect(pos2_t[:, t0 // 16 : t1 // 16]), gate_t[b][:, 1, t0:t1], MULT)
+                if b < 2:
+                    for h0 in range(0, n, 384):
+                        bank = psum.tile([P, SLICE], F32, name="bank")
+                        nc.tensor.matmul(bank[:, :384], lhsT=ident[:], rhs=first[:, h0 : h0 + 384], start=True, stop=False)
+                        nc.tensor.matmul(bank[:, :384], lhsT=ident[:], rhs=second[:, h0 : h0 + 384], start=False, stop=True)
+                        nc.scalar.copy(out=total[:, h0 : h0 + 384], in_=bank[:, :384])
+                else:
+                    nc.vector.tensor_add(total[:], first[:], second[:])
+                nc.scalar.dma_start(out[b * P : (b + 1) * P, t0:t1], total[:])

@@ -22,9 +22,7 @@ BLOCKS = N // P
 X_CHUNKS = ((0, 512), (512, 768))
 SLICE = 512
 SLICES = SLOTS // SLICE
-W_LOADS_A = ((0, 2, 0, 3), (2, 4, 0, 3), (4, 6, 0, 3), (6, 12, 0, 1))
-W_LOADS_B = ((6, 12, 1, 2),)
-W_LOADS_C = ((6, 12, 2, 3),)
+W_LOADS = ((0, 3, 0, 3), (3, 6, 0, 3), (6, 9, 0, 3), (9, 12, 0, 1), (9, 12, 1, 3))
 
 
 def tile_routed_moe_kernel(tc, xT, w_words, w_scales, gate, offs, pos1, pos2, out):
@@ -42,55 +40,30 @@ def tile_routed_moe_kernel(tc, xT, w_words, w_scales, gate, offs, pos1, pos2, ou
         x_bytes = keep.tile([P, T], U8, name="x_bytes", align_bytes=64)
         nc.gpsimd.memset(x_bytes[:], 0)
         w_bytes = keep.tile([P, E * PASSES, N], U8, name="w_bytes", align_bytes=64)
-        nc.gpsimd.memset(w_bytes[:].rearrange("p a n -> p (a n)").bitcast(I32), 0)
+        nc.vector.memset(w_bytes[:].rearrange("p a n -> p (a n)").bitcast(I32), 0)
 
         ident = keep.tile([P, P], F32, name="ident")
         make_identity(nc, ident[:])
 
+        stage = ctx.enter_context(tc.tile_pool(name="stage", bufs=4))
+        late = ctx.enter_context(tc.tile_pool(name="late", bufs=1))
         raw = {}
         for a in range(PASSES):
             rows = xT[a * 512 : (a + 1) * 512, :].rearrange("(p t) n -> p t n", t=4)
             for c, (c0, c1) in enumerate(X_CHUNKS):
-                raw[a, c] = keep.tile([P, 4, c1 - c0], F32, name=f"raw_{a}_{c}")
+                raw[a, c] = stage.tile([P, 4, c1 - c0], F32, name=f"raw_{a}_{c}", tag="stage", align_bytes=64)
                 nc.sync.dma_start(raw[a, c][:], rows[:, :, c0:c1])
             if a == 0:
                 nc.sync.dma_start(offs_t[:], offs)
 
-        for q in range(4):
+        for i in range(4):
             nc.sync.dma_start(
-                w_bytes[32 * q : 32 * q + 4, :, :].bitcast(I32),
-                w_scales[:, :, 4 * q : 4 * q + 4, :].rearrange("e a q n -> q (e a) n").bitcast(I32),
+                w_bytes[i:P:32, :, :].bitcast(I32),
+                w_scales[:, :, i:16:4, :].rearrange("e a q n -> q (e a) n").bitcast(I32),
             )
 
-        w_at = {}
-
-        def load_weights(loads):
-            for e0, e1, b0, b1 in loads:
-                w = keep.tile([P, (e1 - e0) * PASSES, (b1 - b0) * P * 4], U8, name=f"w_{e0}_{b0}", align_bytes=64)
-                nc.sync.dma_start(
-                    w[:], w_words[e0:e1, :, :, b0 * P : b1 * P, :].rearrange("e a p n r -> p (e a) (n r)")
-                )
-                for e in range(e0, e1):
-                    for b in range(b0, b1):
-                        w_at[e, b] = (w, (e - e0) * PASSES, (b - b0) * P * 4)
-
-        gate_t = {}
-
-        def load_gate(b):
-            gate_t[b] = keep.tile([P, 2, T], F32, name=f"gate_{b}")
-            nc.sync.dma_start(gate_t[b][:], gate[:, b * P : (b + 1) * P, :].rearrange("s p t -> p s t"))
-
-        load_weights(W_LOADS_A)
-        nc.sync.dma_start(pos1_t[:], pos1)
-        nc.sync.dma_start(pos2_t[:], pos2)
-        load_gate(0)
-        load_weights(W_LOADS_B)
-        load_gate(1)
-        load_weights(W_LOADS_C)
-        load_gate(2)
-
-        x_words = [keep.tile([P, T], U32, name=f"x_words_{a}", align_bytes=64) for a in range(PASSES)]
-        inter = [keep.tile([P, T, 4], BF16, name=f"inter_{a}", align_bytes=64) for a in range(PASSES)]
+        x_words = [late.tile([P, T], U32, name=f"x_words_{a}", tag=f"x_words_{a}", align_bytes=64) for a in range(PASSES)]
+        inter = [late.tile([P, T, 4], BF16, name=f"inter_{a}", tag=f"inter_{a}", align_bytes=64) for a in range(PASSES)]
 
         def interleave(engine, a, c, lo, hi):
             c0 = X_CHUNKS[c][0]
@@ -108,6 +81,24 @@ def tile_routed_moe_kernel(tc, xT, w_words, w_scales, gate, offs, pos1, pos2, ou
                 scales=x_bytes[4 * a : P, c0:c1],
                 in_=inter[a][:, c0:c1, :].rearrange("p n t -> p (n t)"),
             )
+
+        w_at = {}
+
+        def load_weights(pool, tag, e0, e1, b0, b1):
+            w = pool.tile([P, (e1 - e0) * PASSES, (b1 - b0) * P * 4], U8, name=f"w_{e0}_{b0}", tag=tag, align_bytes=64)
+            nc.sync.dma_start(
+                w[:].bitcast(I32),
+                w_words[e0:e1, :, :, b0 * P : b1 * P, :].rearrange("e a p n r -> p (e a) (n r)").bitcast(I32),
+            )
+            for e in range(e0, e1):
+                for b in range(b0, b1):
+                    w_at[e, b] = (w, (e - e0) * PASSES, (b - b0) * P * 4)
+
+        gate_t = {}
+
+        def load_gate(b, tag):
+            gate_t[b] = late.tile([P, 2, T], F32, name=f"gate_{b}", tag=tag, align_bytes=64)
+            nc.sync.dma_start(gate_t[b][:], gate[:, b * P : (b + 1) * P, :].rearrange("s p t -> p s t"))
 
         s_words = {}
         s_bytes = {}
@@ -139,28 +130,42 @@ def tile_routed_moe_kernel(tc, xT, w_words, w_scales, gate, offs, pos1, pos2, ou
         quantise(1, 0)
         quantise(1, 1)
 
+        for load in W_LOADS[:4]:
+            load_weights(stage, "stage", *load)
+        nc.sync.dma_start(pos1_t[:], pos1)
+        nc.sync.dma_start(pos2_t[:], pos2)
+        load_gate(0, "inter_0")
+        load_weights(late, "inter_1", *W_LOADS[4])
+        load_gate(1, "x_words_0")
+        load_gate(2, "x_words_1")
+
         sums = [keep.tile([P, SLOTS], F32, name=f"sums_{b}") for b in range(BLOCKS)]
+
+        def multiply(s, b):
+            bank = psum.tile([P, SLICE], F32, name="bank")
+            for i in range(SLICE // C):
+                e = s * (SLICE // C) + i
+                w, row, col = w_at[e, b]
+                cols = slice(i * C, (i + 1) * C)
+                for a in range(PASSES):
+                    nc.tensor.matmul_mx(
+                        out=bank[:, cols],
+                        lhsT=w[:, row + a, col : col + 4 * P].bitcast(FP8X4),
+                        lhsT_scale=w_bytes[:, 2 * e + a, b * P : (b + 1) * P],
+                        rhs=s_words[a, s][:, cols].bitcast(FP8X4),
+                        rhs_scale=s_bytes[s][4 * a : P, cols],
+                        start=(a == 0),
+                        stop=(a == PASSES - 1),
+                    )
+            nc.scalar.copy(out=sums[b][:, s * SLICE : (s + 1) * SLICE], in_=bank[:])
 
         for s in range(SLICES):
             gather_bytes(s)
             gather_words(1, s)
-            for b in range(BLOCKS):
-                bank = psum.tile([P, SLICE], F32, name="bank")
-                for i in range(SLICE // C):
-                    e = s * (SLICE // C) + i
-                    w, row, col = w_at[e, b]
-                    cols = slice(i * C, (i + 1) * C)
-                    for a in range(PASSES):
-                        nc.tensor.matmul_mx(
-                            out=bank[:, cols],
-                            lhsT=w[:, row + a, col : col + 4 * P].bitcast(FP8X4),
-                            lhsT_scale=w_bytes[:, 2 * e + a, b * P : (b + 1) * P],
-                            rhs=s_words[a, s][:, cols].bitcast(FP8X4),
-                            rhs_scale=s_bytes[s][4 * a : P, cols],
-                            start=(a == 0),
-                            stop=(a == PASSES - 1),
-                        )
-                nc.scalar.copy(out=sums[b][:, s * SLICE : (s + 1) * SLICE], in_=bank[:])
+            multiply(s, 0)
+        for b in range(1, BLOCKS):
+            for s in range(SLICES):
+                multiply(s, b)
 
         PIECES = {0: (0, 768), 1: (0, 768), 2: (0, 384, 768)}
         for b in range(BLOCKS):

@@ -19,10 +19,9 @@ MULT = mybir.AluOpType.mult
 
 PASSES = 2
 BLOCKS = N // P
-X_CHUNKS = ((0, 512), (512, 768))
+CHUNKS = ((0, 512), (512, 768))
 SLICE = 512
 SLICES = SLOTS // SLICE
-W_LOADS = ((0, 3, 0, 3), (3, 6, 0, 3), (6, 9, 0, 3), (9, 12, 0, 1), (9, 12, 1, 3))
 
 
 def tile_routed_moe_kernel(tc, xT, w_words, w_scales, gate, offs, pos1, pos2, out):
@@ -30,62 +29,43 @@ def tile_routed_moe_kernel(tc, xT, w_words, w_scales, gate, offs, pos1, pos2, ou
     with ExitStack() as ctx:
         lists = ctx.enter_context(tc.tile_pool(name="lists", bufs=1))
         keep = ctx.enter_context(tc.tile_pool(name="keep", bufs=1))
-        work = ctx.enter_context(tc.tile_pool(name="work", bufs=3))
+        ring = ctx.enter_context(tc.tile_pool(name="ring", bufs=1))
+        work = ctx.enter_context(tc.tile_pool(name="work", bufs=2))
         psum = ctx.enter_context(tc.psum_pool(name="psum", bufs=8))
 
         offs_t = lists.tile([P, SLOTS // 16], U16, name="offs_t")
         pos1_t = lists.tile([P, T // 16], U16, name="pos1_t")
         pos2_t = lists.tile([P, T // 16], U16, name="pos2_t")
 
-        x_bytes = keep.tile([P, T], U8, name="x_bytes", align_bytes=64)
-        nc.gpsimd.memset(x_bytes[:], 0)
+        x_bytes = ring.tile([P, T], U8, name="x_bytes", tag="x_bytes", align_bytes=64)
         w_bytes = keep.tile([P, E * PASSES, N], U8, name="w_bytes", align_bytes=64)
-        nc.vector.memset(w_bytes[:].rearrange("p a n -> p (a n)").bitcast(I32), 0)
+        nc.vector.memset(w_bytes[:, :E, :].rearrange("p a n -> p (a n)").bitcast(I32), 0)
+        nc.gpsimd.memset(w_bytes[:, E:, :].rearrange("p a n -> p (a n)").bitcast(I32), 0)
+        nc.gpsimd.memset(x_bytes[:].bitcast(I32), 0)
 
-        ident = keep.tile([P, P], F32, name="ident")
-        make_identity(nc, ident[:])
-
-        stage = ctx.enter_context(tc.tile_pool(name="stage", bufs=4))
-        late = ctx.enter_context(tc.tile_pool(name="late", bufs=1))
         raw = {}
         for a in range(PASSES):
             rows = xT[a * 512 : (a + 1) * 512, :].rearrange("(p t) n -> p t n", t=4)
-            for c, (c0, c1) in enumerate(X_CHUNKS):
-                raw[a, c] = stage.tile([P, 4, c1 - c0], F32, name=f"raw_{a}_{c}", tag="stage", align_bytes=64)
+            for c, (c0, c1) in enumerate(CHUNKS):
+                raw[a, c] = ring.tile([P, 4, c1 - c0], F32, name=f"raw_{a}_{c}", tag=f"raw_{a}_{c}", align_bytes=64)
                 nc.sync.dma_start(raw[a, c][:], rows[:, :, c0:c1])
             if a == 0:
                 nc.sync.dma_start(offs_t[:], offs)
+        nc.sync.dma_start(pos1_t[:], pos1)
+        nc.sync.dma_start(pos2_t[:], pos2)
 
         for i in range(4):
-            nc.sync.dma_start(
-                w_bytes[i:P:32, :, :].bitcast(I32),
-                w_scales[:, :, i:16:4, :].rearrange("e a q n -> q (e a) n").bitcast(I32),
+            nc.gpsimd.dma_start(
+                w_bytes[i:P:32, :, :].bitcast(F32),
+                w_scales[:, :, i:16:4, :].rearrange("e a q n -> q (e a) n").bitcast(F32),
             )
-
-        x_words = [late.tile([P, T], U32, name=f"x_words_{a}", tag=f"x_words_{a}", align_bytes=64) for a in range(PASSES)]
-        inter = [late.tile([P, T, 4], BF16, name=f"inter_{a}", tag=f"inter_{a}", align_bytes=64) for a in range(PASSES)]
-
-        def interleave(engine, a, c, lo, hi):
-            c0 = X_CHUNKS[c][0]
-            dst = inter[a][:, c0 + lo : c0 + hi, :]
-            src = raw[a, c][:, :, lo:hi].rearrange("p t n -> p n t")
-            if engine == "scalar":
-                nc.scalar.copy(out=dst, in_=src)
-            else:
-                nc.vector.tensor_copy(out=dst, in_=src)
-
-        def quantise(a, c):
-            c0, c1 = X_CHUNKS[c]
-            nc.vector.quantize_mx(
-                out=x_words[a][:, c0:c1].bitcast(FP8X4),
-                scales=x_bytes[4 * a : P, c0:c1],
-                in_=inter[a][:, c0:c1, :].rearrange("p n t -> p (n t)"),
-            )
+        ident = keep.tile([P, P], F32, name="ident")
+        make_identity(nc, ident[:])
 
         w_at = {}
 
-        def load_weights(pool, tag, e0, e1, b0, b1):
-            w = pool.tile([P, (e1 - e0) * PASSES, (b1 - b0) * P * 4], U8, name=f"w_{e0}_{b0}", tag=tag, align_bytes=64)
+        def load_weights(tag, e0, e1, b0, b1):
+            w = ring.tile([P, (e1 - e0) * PASSES, (b1 - b0) * P * 4], U8, name=f"w_{e0}_{b0}", tag=tag, align_bytes=64)
             nc.sync.dma_start(
                 w[:].bitcast(I32),
                 w_words[e0:e1, :, :, b0 * P : b1 * P, :].rearrange("e a p n r -> p (e a) (n r)").bitcast(I32),
@@ -94,95 +74,129 @@ def tile_routed_moe_kernel(tc, xT, w_words, w_scales, gate, offs, pos1, pos2, ou
                 for b in range(b0, b1):
                     w_at[e, b] = (w, (e - e0) * PASSES, (b - b0) * P * 4)
 
-        gate_t = {}
+        gates = {}
 
-        def load_gate(b, tag):
-            gate_t[b] = late.tile([P, 2, T], F32, name=f"gate_{b}", tag=tag, align_bytes=64)
-            nc.sync.dma_start(gate_t[b][:], gate[:, b * P : (b + 1) * P, :].rearrange("s p t -> p s t"))
+        def load_gate(tag, b):
+            gates[b] = ring.tile([P, 2, T], F32, name=f"gate_{b}", tag=tag, align_bytes=64)
+            nc.sync.dma_start(gates[b][:], gate[:, b * P : (b + 1) * P, :].rearrange("s p t -> p s t"))
 
-        s_words = {}
-        s_bytes = {}
+        x_words, inter = [], []
+        for a in range(PASSES):
+            x_words.append(ring.tile([P, T], U32, name=f"x_words_{a}", tag=f"x_words_{a}", align_bytes=64))
+            inter.append(ring.tile([P, T, 4], BF16, name=f"inter_{a}", tag=f"inter_{a}", align_bytes=64))
 
-        def gather_words(a, s):
-            s_words[a, s] = keep.tile([P, SLICE], U32, name=f"s_words_{a}_{s}", align_bytes=64)
-            nc.vector.tensor_copy(
-                s_words[a, s][:], x_words[a][:].indirect(offs_t[:, s * SLICE // 16 : (s + 1) * SLICE // 16])
+        def interleave(copy, a, c, lo, hi):
+            c0 = CHUNKS[c][0]
+            copy(out=inter[a][:, c0 + lo : c0 + hi, :], in_=raw[a, c][:, :, lo:hi].rearrange("p t n -> p n t"))
+
+        def quantise(a, c):
+            c0, c1 = CHUNKS[c]
+            nc.vector.quantize_mx(
+                out=x_words[a][:, c0:c1].bitcast(FP8X4),
+                scales=x_bytes[4 * a : P, c0:c1],
+                in_=inter[a][:, c0:c1, :].rearrange("p n t -> p (n t)"),
             )
+
+        words = {}
+        bytes_of = {}
+
+        def gather_words(a, s, lo, hi):
+            g = ring.tile([P, hi - lo], U32, name=f"words_{a}_{s}_{lo}", tag=f"words_{a}_{s}_{lo}", align_bytes=64)
+            first = s * SLICE + lo
+            nc.vector.tensor_copy(g[:], x_words[a][:].indirect(offs_t[:, first // 16 : (first + hi - lo) // 16]))
+            for j in range(lo, hi, C):
+                words[a, (s * SLICE + j) // C] = (g, j - lo)
 
         def gather_bytes(s):
-            s_bytes[s] = keep.tile([P, SLICE], U8, name=f"s_bytes_{s}", align_bytes=64)
+            bytes_of[s] = keep.tile([P, SLICE], U8, name=f"bytes_{s}", align_bytes=64)
             nc.vector.tensor_copy(
-                s_bytes[s][:], x_bytes[:].indirect(offs_t[:, s * SLICE // 16 : (s + 1) * SLICE // 16])
+                bytes_of[s][:], x_bytes[:].indirect(offs_t[:, s * SLICE // 16 : (s + 1) * SLICE // 16])
             )
-
-        interleave("scalar", 0, 0, 0, 192)
-        interleave("vector", 0, 0, 192, 512)
-        interleave("scalar", 0, 1, 0, 96)
-        quantise(0, 0)
-        interleave("vector", 0, 1, 96, 256)
-        quantise(0, 1)
-        interleave("scalar", 1, 0, 0, 256)
-        interleave("scalar", 1, 0, 256, 512)
-        for s in range(SLICES):
-            gather_words(0, s)
-        interleave("scalar", 1, 1, 0, 128)
-        interleave("vector", 1, 1, 128, 256)
-        quantise(1, 0)
-        quantise(1, 1)
-
-        for load in W_LOADS[:4]:
-            load_weights(stage, "stage", *load)
-        nc.sync.dma_start(pos1_t[:], pos1)
-        nc.sync.dma_start(pos2_t[:], pos2)
-        load_gate(0, "inter_0")
-        load_weights(late, "inter_1", *W_LOADS[4])
-        load_gate(1, "x_words_0")
-        load_gate(2, "x_words_1")
 
         sums = [keep.tile([P, SLOTS], F32, name=f"sums_{b}") for b in range(BLOCKS)]
 
-        def multiply(s, b):
+        def multiply(e0, e1, b):
             bank = psum.tile([P, SLICE], F32, name="bank")
-            for i in range(SLICE // C):
-                e = s * (SLICE // C) + i
+            for e in range(e0, e1):
                 w, row, col = w_at[e, b]
-                cols = slice(i * C, (i + 1) * C)
+                s, j = divmod(e * C, SLICE)
+                cols = slice((e - e0) * C, (e - e0 + 1) * C)
                 for a in range(PASSES):
+                    g, g0 = words[a, e]
                     nc.tensor.matmul_mx(
                         out=bank[:, cols],
                         lhsT=w[:, row + a, col : col + 4 * P].bitcast(FP8X4),
                         lhsT_scale=w_bytes[:, 2 * e + a, b * P : (b + 1) * P],
-                        rhs=s_words[a, s][:, cols].bitcast(FP8X4),
-                        rhs_scale=s_bytes[s][4 * a : P, cols],
+                        rhs=g[:, g0 : g0 + C].bitcast(FP8X4),
+                        rhs_scale=bytes_of[s][4 * a : P, j : j + C],
                         start=(a == 0),
                         stop=(a == PASSES - 1),
                     )
-            nc.scalar.copy(out=sums[b][:, s * SLICE : (s + 1) * SLICE], in_=bank[:])
+            nc.scalar.copy(out=sums[b][:, e0 * C : e1 * C], in_=bank[:, : (e1 - e0) * C])
+
+        vcopy, scopy = nc.vector.tensor_copy, nc.scalar.copy
+        interleave(scopy, 0, 0, 0, 192)
+        interleave(vcopy, 0, 0, 192, 512)
+        interleave(scopy, 0, 1, 0, 96)
+        quantise(0, 0)
+        interleave(vcopy, 0, 1, 96, 256)
+        quantise(0, 1)
+        interleave(scopy, 1, 0, 0, 256)
+        interleave(scopy, 1, 0, 256, 512)
+        for s in range(SLICES):
+            gather_words(0, s, 0, SLICE)
+        interleave(scopy, 1, 1, 0, 128)
+        interleave(vcopy, 1, 1, 128, 256)
+        quantise(1, 0)
+        quantise(1, 1)
+
+        load_weights("raw_0_0", 0, 2, 0, 3)
+        load_weights("raw_0_1", 2, 4, 0, 3)
+        load_weights("inter_0", 4, 12, 0, 1)
+        load_gate("raw_1_0", 0)
+        load_weights("raw_1_1", 4, 12, 1, 2)
+        load_gate("inter_1", 1)
 
         for s in range(SLICES):
             gather_bytes(s)
-            gather_words(1, s)
-            multiply(s, 0)
+            if s < SLICES - 1:
+                gather_words(1, s, 0, SLICE)
+                multiply(4 * s, 4 * s + 4, 0)
+            else:
+                gather_words(1, s, 0, 384)
+                multiply(4 * s, 4 * s + 3, 0)
+                gather_words(1, s, 384, 512)
+                multiply(4 * s + 3, 4 * s + 4, 0)
+        load_weights("x_bytes", 4, 12, 2, 3)
+        load_gate("x_words_1", 2)
         for b in range(1, BLOCKS):
             for s in range(SLICES):
-                multiply(s, b)
+                multiply(4 * s, 4 * s + 4, b)
 
-        PIECES = {0: (0, 768), 1: (0, 768), 2: (0, 384, 768)}
-        for b in range(BLOCKS):
-            edges = PIECES[b]
-            for t0, t1 in zip(edges[:-1], edges[1:]):
-                n = t1 - t0
-                first = work.tile([P, n], F32, name=f"first_{n}")
-                second = work.tile([P, n], F32, name=f"second_{n}")
-                total = work.tile([P, n], F32, name=f"total_{n}")
-                nc.vector.tensor_tensor(first[:], sums[b][:].indirect(pos1_t[:, t0 // 16 : t1 // 16]), gate_t[b][:, 0, t0:t1], MULT)
-                nc.vector.tensor_tensor(second[:], sums[b][:].indirect(pos2_t[:, t0 // 16 : t1 // 16]), gate_t[b][:, 1, t0:t1], MULT)
-                if b < 2:
-                    for h0 in range(0, n, 384):
-                        bank = psum.tile([P, SLICE], F32, name="bank")
-                        nc.tensor.matmul(bank[:, :384], lhsT=ident[:], rhs=first[:, h0 : h0 + 384], start=True, stop=False)
-                        nc.tensor.matmul(bank[:, :384], lhsT=ident[:], rhs=second[:, h0 : h0 + 384], start=False, stop=True)
-                        nc.scalar.copy(out=total[:, h0 : h0 + 384], in_=bank[:, :384])
-                else:
-                    nc.vector.tensor_add(total[:], first[:], second[:])
-                nc.scalar.dma_start(out[b * P : (b + 1) * P, t0:t1], total[:])
+        def gathered(b, which, pos, t0, t1):
+            g = work.tile([P, t1 - t0], F32, name=f"g{which}_{t1 - t0}")
+            nc.vector.tensor_tensor(g[:], sums[b][:].indirect(pos[:, t0 // 16 : t1 // 16]), gates[b][:, which, t0:t1], MULT)
+            return g
+
+        HALF = T // 2
+        for b in range(BLOCKS - 1):
+            total = work.tile([P, T], F32, name="total")
+            first = gathered(b, 0, pos1_t, 0, T)
+            banks = []
+            for h in range(2):
+                bank = psum.tile([P, SLICE], F32, name="bank")
+                nc.tensor.matmul(bank[:, :HALF], lhsT=ident[:], rhs=first[:, h * HALF : (h + 1) * HALF], start=True, stop=False)
+                banks.append(bank)
+            second = gathered(b, 1, pos2_t, 0, T)
+            for h in range(2):
+                cols = slice(h * HALF, (h + 1) * HALF)
+                nc.tensor.matmul(banks[h][:, :HALF], lhsT=ident[:], rhs=second[:, cols], start=False, stop=True)
+                nc.scalar.copy(out=total[:, cols], in_=banks[h][:, :HALF])
+            nc.scalar.dma_start(out[b * P : (b + 1) * P, :], total[:])
+        b = BLOCKS - 1
+        for t0, t1 in ((0, 512), (512, 768)):
+            total = work.tile([P, t1 - t0], F32, name=f"total_{t1 - t0}")
+            first = gathered(b, 0, pos1_t, t0, t1)
+            second = gathered(b, 1, pos2_t, t0, t1)
+            nc.vector.tensor_add(total[:], first[:], second[:])
+            nc.sync.dma_start(out[b * P : (b + 1) * P, t0:t1], total[:])

from contextlib import ExitStack

import concourse.mybir as mybir
from concourse.masks import make_identity

K, T, E, C, N = 1024, 768, 12, 128, 384
SLOTS = E * C
P = 128
FLOPS = 2 * K * N * SLOTS

F32 = mybir.dt.float32
BF16 = mybir.dt.bfloat16
I32 = mybir.dt.int32
U32 = mybir.dt.uint32
U16 = mybir.dt.uint16
U8 = mybir.dt.uint8
FP8X4 = mybir.dt.float8_e4m3fn_x4
MULT = mybir.AluOpType.mult

PASSES = 2
BLOCKS = N // P
CHUNKS = ((0, 512), (512, 768))
SLICE = 512
SLICES = SLOTS // SLICE


def tile_routed_moe_kernel(tc, xT, w_words, w_scales, gate, offs, pos1, pos2, out):
    nc = tc.nc
    with ExitStack() as ctx:
        lists = ctx.enter_context(tc.tile_pool(name="lists", bufs=1))
        keep = ctx.enter_context(tc.tile_pool(name="keep", bufs=1))
        ring = ctx.enter_context(tc.tile_pool(name="ring", bufs=1))
        work = ctx.enter_context(tc.tile_pool(name="work", bufs=2))
        psum = ctx.enter_context(tc.psum_pool(name="psum", bufs=8))

        offs_t = lists.tile([P, SLOTS // 16], U16, name="offs_t")
        pos1_t = lists.tile([P, T // 16], U16, name="pos1_t")
        pos2_t = lists.tile([P, T // 16], U16, name="pos2_t")

        x_bytes = ring.tile([P, T], U8, name="x_bytes", tag="x_bytes", align_bytes=64)
        w_bytes = keep.tile([P, E * PASSES, N], U8, name="w_bytes", align_bytes=64)
        nc.vector.memset(w_bytes[:, :E, :].rearrange("p a n -> p (a n)").bitcast(I32), 0)
        nc.gpsimd.memset(w_bytes[:, E:, :].rearrange("p a n -> p (a n)").bitcast(I32), 0)
        nc.gpsimd.memset(x_bytes[:].bitcast(I32), 0)

        raw = {}
        for a in range(PASSES):
            rows = xT[a * 512 : (a + 1) * 512, :].rearrange("(p t) n -> p t n", t=4)
            for c, (c0, c1) in enumerate(CHUNKS):
                raw[a, c] = ring.tile([P, 4, c1 - c0], F32, name=f"raw_{a}_{c}", tag=f"raw_{a}_{c}", align_bytes=64)
                nc.sync.dma_start(raw[a, c][:], rows[:, :, c0:c1])
            if a == 0:
                nc.sync.dma_start(offs_t[:], offs)
        nc.sync.dma_start(pos1_t[:], pos1)
        nc.sync.dma_start(pos2_t[:], pos2)

        for i in range(4):
            nc.gpsimd.dma_start(
                w_bytes[i:P:32, :, :].bitcast(F32),
                w_scales[:, :, i:16:4, :].rearrange("e a q n -> q (e a) n").bitcast(F32),
            )
        ident = keep.tile([P, P], F32, name="ident")
        make_identity(nc, ident[:])

        w_at = {}

        def load_weights(tag, e0, e1, b0, b1):
            w = ring.tile([P, (e1 - e0) * PASSES, (b1 - b0) * P * 4], U8, name=f"w_{e0}_{b0}", tag=tag, align_bytes=64)
            nc.sync.dma_start(
                w[:].bitcast(I32),
                w_words[e0:e1, :, :, b0 * P : b1 * P, :].rearrange("e a p n r -> p (e a) (n r)").bitcast(I32),
            )
            for e in range(e0, e1):
                for b in range(b0, b1):
                    w_at[e, b] = (w, (e - e0) * PASSES, (b - b0) * P * 4)

        gates = {}

        def load_gate(tag, b):
            gates[b] = ring.tile([P, 2, T], F32, name=f"gate_{b}", tag=tag, align_bytes=64)
            nc.sync.dma_start(gates[b][:], gate[:, b * P : (b + 1) * P, :].rearrange("s p t -> p s t"))

        x_words, inter = [], []
        for a in range(PASSES):
            x_words.append(ring.tile([P, T], U32, name=f"x_words_{a}", tag=f"x_words_{a}", align_bytes=64))
            inter.append(ring.tile([P, T, 4], BF16, name=f"inter_{a}", tag=f"inter_{a}", align_bytes=64))

        def interleave(copy, a, c, lo, hi):
            c0 = CHUNKS[c][0]
            copy(out=inter[a][:, c0 + lo : c0 + hi, :], in_=raw[a, c][:, :, lo:hi].rearrange("p t n -> p n t"))

        def quantise(a, c):
            c0, c1 = CHUNKS[c]
            nc.vector.quantize_mx(
                out=x_words[a][:, c0:c1].bitcast(FP8X4),
                scales=x_bytes[4 * a : P, c0:c1],
                in_=inter[a][:, c0:c1, :].rearrange("p n t -> p (n t)"),
            )

        words = {}
        bytes_of = {}

        def gather_words(a, s, lo, hi):
            g = ring.tile([P, hi - lo], U32, name=f"words_{a}_{s}_{lo}", tag=f"words_{a}_{s}_{lo}", align_bytes=64)
            first = s * SLICE + lo
            nc.vector.tensor_copy(g[:], x_words[a][:].indirect(offs_t[:, first // 16 : (first + hi - lo) // 16]))
            for j in range(lo, hi, C):
                words[a, (s * SLICE + j) // C] = (g, j - lo)

        def gather_bytes(s):
            bytes_of[s] = keep.tile([P, SLICE], U8, name=f"bytes_{s}", align_bytes=64)
            nc.vector.tensor_copy(
                bytes_of[s][:], x_bytes[:].indirect(offs_t[:, s * SLICE // 16 : (s + 1) * SLICE // 16])
            )

        sums = [keep.tile([P, SLOTS], F32, name=f"sums_{b}") for b in range(BLOCKS)]

        def multiply(e0, e1, b):
            bank = psum.tile([P, SLICE], F32, name="bank")
            for e in range(e0, e1):
                w, row, col = w_at[e, b]
                s, j = divmod(e * C, SLICE)
                cols = slice((e - e0) * C, (e - e0 + 1) * C)
                for a in range(PASSES):
                    g, g0 = words[a, e]
                    nc.tensor.matmul_mx(
                        out=bank[:, cols],
                        lhsT=w[:, row + a, col : col + 4 * P].bitcast(FP8X4),
                        lhsT_scale=w_bytes[:, 2 * e + a, b * P : (b + 1) * P],
                        rhs=g[:, g0 : g0 + C].bitcast(FP8X4),
                        rhs_scale=bytes_of[s][4 * a : P, j : j + C],
                        start=(a == 0),
                        stop=(a == PASSES - 1),
                    )
            nc.scalar.copy(out=sums[b][:, e0 * C : e1 * C], in_=bank[:, : (e1 - e0) * C])

        vcopy, scopy = nc.vector.tensor_copy, nc.scalar.copy
        interleave(scopy, 0, 0, 0, 192)
        interleave(vcopy, 0, 0, 192, 512)
        interleave(scopy, 0, 1, 0, 96)
        quantise(0, 0)
        interleave(vcopy, 0, 1, 96, 256)
        quantise(0, 1)
        interleave(scopy, 1, 0, 0, 256)
        interleave(scopy, 1, 0, 256, 512)
        for s in range(SLICES):
            gather_words(0, s, 0, SLICE)
        interleave(scopy, 1, 1, 0, 128)
        interleave(vcopy, 1, 1, 128, 256)
        quantise(1, 0)
        quantise(1, 1)

        load_weights("raw_0_0", 0, 2, 0, 3)
        load_weights("raw_0_1", 2, 4, 0, 3)
        load_weights("inter_0", 4, 12, 0, 1)
        load_gate("raw_1_0", 0)
        load_weights("raw_1_1", 4, 12, 1, 2)
        load_gate("inter_1", 1)

        for s in range(SLICES):
            gather_bytes(s)
            if s < SLICES - 1:
                gather_words(1, s, 0, SLICE)
                multiply(4 * s, 4 * s + 4, 0)
            else:
                gather_words(1, s, 0, 384)
                multiply(4 * s, 4 * s + 3, 0)
                gather_words(1, s, 384, 512)
                multiply(4 * s + 3, 4 * s + 4, 0)
        load_weights("x_bytes", 4, 12, 2, 3)
        load_gate("x_words_1", 2)
        for b in range(1, BLOCKS):
            for s in range(SLICES):
                multiply(4 * s, 4 * s + 4, b)

        def gathered(b, which, pos, t0, t1):
            g = work.tile([P, t1 - t0], F32, name=f"g{which}_{t1 - t0}")
            nc.vector.tensor_tensor(g[:], sums[b][:].indirect(pos[:, t0 // 16 : t1 // 16]), gates[b][:, which, t0:t1], MULT)
            return g

        HALF = T // 2
        for b in range(BLOCKS - 1):
            total = work.tile([P, T], F32, name="total")
            first = gathered(b, 0, pos1_t, 0, T)
            banks = []
            for h in range(2):
                bank = psum.tile([P, SLICE], F32, name="bank")
                nc.tensor.matmul(bank[:, :HALF], lhsT=ident[:], rhs=first[:, h * HALF : (h + 1) * HALF], start=True, stop=False)
                banks.append(bank)
            second = gathered(b, 1, pos2_t, 0, T)
            for h in range(2):
                cols = slice(h * HALF, (h + 1) * HALF)
                nc.tensor.matmul(banks[h][:, :HALF], lhsT=ident[:], rhs=second[:, cols], start=False, stop=True)
                nc.scalar.copy(out=total[:, cols], in_=banks[h][:, :HALF])
            nc.scalar.dma_start(out[b * P : (b + 1) * P, :], total[:])
        b = BLOCKS - 1
        for t0, t1 in ((0, 512), (512, 768)):
            total = work.tile([P, t1 - t0], F32, name=f"total_{t1 - t0}")
            first = gathered(b, 0, pos1_t, t0, t1)
            second = gathered(b, 1, pos2_t, t0, t1)
            nc.vector.tensor_add(total[:], first[:], second[:])
            nc.sync.dma_start(out[b * P : (b + 1) * P, t0:t1], total[:])
